import numpy as np
import ml_dtypes


def mxq(x, axis, fmt="e4m3"):
    dtype, down = {"e4m3": (ml_dtypes.float8_e4m3fn, 7), "e5m2": (ml_dtypes.float8_e5m2, 14)}[fmt]
    v = np.moveaxis(np.asarray(x, np.float32).astype(ml_dtypes.bfloat16).astype(np.float64), axis, -1)
    blocks = v.reshape(v.shape[:-1] + (-1, 32))
    amax = np.abs(blocks).max(-1, keepdims=True)
    byte = np.maximum(np.where(amax > 0, np.frexp(amax)[1] - 1 + 127, 0) - down, 1)
    scale = np.exp2(byte - 127.0)
    codes = (blocks / scale).astype(np.float32).astype(dtype).astype(np.float64)
    return np.moveaxis((codes * scale).reshape(v.shape), -1, axis)


WIDE = False


def mx_kscale(k):
    if not WIDE:
        return np.ones(k)
    levels = np.array([10, -10, 5, -5, 0])
    if k % 512:
        return np.exp2(np.random.permutation(np.resize(levels, k // 32))).repeat(32)
    a = np.empty((k // 512, 16))
    for p in range(k // 512):
        a[p, :8] = np.random.permutation(np.resize(levels, 8))
        for g in range(8):
            far = levels[np.abs(levels - a[p, g]) >= 10]
            a[p, g + 8] = far[np.random.randint(len(far))]
    return np.exp2(a.ravel()).repeat(32)


def f64(x):
    return np.asarray(x).astype(np.float64)


def striped(idx):
    return np.tile(idx.reshape(-1, 16).T, (8, 1)).astype(np.uint16)


def unstriped(offs):
    return offs[:16].T.reshape(-1).astype(np.int64)


E2M1 = np.array([0.0, 0.5, 1.0, 1.5, 2.0, 3.0, 4.0, 6.0, -0.0, -0.5, -1.0, -1.5, -2.0, -3.0, -4.0, -6.0])


def pack_weight(w, fmt):
    k, n = w.shape
    w = f64(np.asarray(w, np.float32).astype(ml_dtypes.bfloat16)).reshape(k // 32, 32, n)
    amax = np.abs(w).max(1)
    if fmt == "e4m3":
        byte = np.frexp(amax)[1] - 1 + 127 - 7
    else:
        mant, ex = np.frexp(amax / 6.0)
        byte = np.where(mant > 0.5, ex, ex - 1) + 127
    byte = np.clip(np.where(amax > 0, byte, 1), 1, 254)
    scaled = (w * np.exp2(127.0 - byte)[:, None, :]).reshape(k, n).astype(np.float32)
    by_word = np.ascontiguousarray(scaled.reshape(k // 512, 128, 4, n).transpose(0, 1, 3, 2))
    if fmt == "e4m3":
        words = by_word.astype(ml_dtypes.float8_e4m3fn).view(np.uint8)
    else:
        c = by_word.astype(ml_dtypes.float4_e2m1fn).view(np.uint8) & 0xF
        words = (c[..., 0::2] | (c[..., 1::2] << 4)).reshape(k // 512, 128, 2 * n)
    return np.ascontiguousarray(words), np.ascontiguousarray(byte.astype(np.uint8).reshape(k // 512, 16, n))


def unpack_weight(words, scales, fmt):
    g, _, n = scales.shape
    words = np.ascontiguousarray(words).reshape(g, 128, n, -1)
    if fmt == "e4m3":
        vals = words.view(ml_dtypes.float8_e4m3fn).astype(np.float64)
    else:
        nib = np.empty((g, 128, n, 4), np.uint8)
        nib[..., 0::2] = words & 0xF
        nib[..., 1::2] = words >> 4
        vals = E2M1[nib]
    vals = vals * np.repeat(np.exp2(scales.astype(np.float64) - 127.0), 8, axis=1)[..., None]
    return vals.transpose(0, 1, 3, 2).reshape(g * 512, n)


def gelu(v):
    return 0.5 * v * (1.0 + np.tanh(np.sqrt(2.0 / np.pi) * (v + 0.044715 * v**3)))


K, KC, KF, H, N, T, S, P = 1536, 512, 1024, 1024, 512, 4096, 1024, 512

def setup_inputs():
    n = np.random.standard_normal
    s = mx_kscale(K)[:, None]
    u = mx_kscale(H)[:, None]
    tab_words, tab_scales = pack_weight(n((K, T)) * s, "e4m3")
    wc_words, wc_scales = pack_weight(n((KC, H)) / np.sqrt(KC) / s[:KC], "e2m1")
    wb_words, wb_scales = pack_weight(1.5 * n((H, N)) / np.sqrt(H) / u, "e4m3")
    return {
        "tab_words": tab_words, "tab_scales": tab_scales,
        "offs": striped(np.random.permutation(T)[:S]),
        "pos1": striped(np.random.permutation(S)[:P]),
        "pos2": striped(np.random.permutation(S)[:P]),
        "wc_words": wc_words, "wc_scales": wc_scales,
        "wf": (n((KF, H)) / np.sqrt(KF) / s[KC:]).astype(np.float32),
        "gain": (np.exp(0.3 * n(H)) * u[:, 0]).astype(np.float32),
        "base": (0.6 * n((H, P)) * u).astype(np.float32),
        "wa": (n((H, N)) / np.sqrt(H) / u).astype(np.float32),
        "wb_words": wb_words, "wb_scales": wb_scales,
        "shift": (0.5 * n(N)).astype(np.float32),
    }

def reference(tab_words, tab_scales, offs, pos1, pos2, wc_words, wc_scales, wf, gain, base, wa, wb_words, wb_scales, shift):
    v = unpack_weight(tab_words, tab_scales, "e4m3")[:, unstriped(offs)]
    wc = unpack_weight(wc_words, wc_scales, "e2m1")
    wfq = mxq(f64(wf), 0, "e4m3")
    e = wc.T @ v[:KC] + wfq.T @ v[KC:]
    h = f64(gain)[:, None] * np.tanh(e)
    xa = mxq(h[:, unstriped(pos1)] + f64(base), 0, "e4m3")
    xb = mxq(np.abs(h[:, unstriped(pos2)]), 0, "e4m3")
    ya = mxq(f64(wa), 0, "e4m3").T @ xa
    yb = unpack_weight(wb_words, wb_scales, "e4m3").T @ xb
    return np.maximum(ya, yb) + f64(shift)[:, None]

@@ -1,0 +1,324 @@
+from contextlib import ExitStack
+
+import concourse.mybir as mybir
+
+FLOPS = 4294967296
+
+F32 = mybir.dt.float32
+BF16 = mybir.dt.bfloat16
+I32 = mybir.dt.int32
+U32 = mybir.dt.uint32
+U16 = mybir.dt.uint16
+U8 = mybir.dt.uint8
+FP8X4 = mybir.dt.float8_e4m3fn_x4
+FP4X4 = mybir.dt.float4_e2m1fn_x4
+ACT = mybir.ActivationFunctionType
+ALU = mybir.AluOpType
+
+P = 128
+PACK = 4
+KP = 512
+T = 4096
+S = 1024
+M = 512
+N = 512
+GAIN_ENGINE = "VVVVSSSS"
+PIECES = ((0, 256), (256, 128), (384, 128))
+
+
+def tile_list_clot_lysis_scores_kernel(
+    tc, tab_words, tab_scales, offs, pos1, pos2, wc_words, wc_scales, wf, gain, base, wa, wb_words, wb_scales, shift, out
+):
+    nc = tc.nc
+    with ExitStack() as ctx:
+        keep = ctx.enter_context(tc.tile_pool(name="keep", bufs=1))
+        psum = ctx.enter_context(tc.psum_pool(name="psum", bufs=8))
+
+        def sbuf(shape, dtype, name, tag=None, bufs=1):
+            return keep.tile(shape, dtype, name=name, tag=tag or name, bufs=bufs, align_bytes=64)
+
+        def quantise(grouped, codes, scales):
+            nc.vector.quantize_mx(out=codes.bitcast(FP8X4), scales=scales, in_=grouped)
+
+        def cast(engine, dst, src):
+            if engine == "S":
+                nc.scalar.copy(out=dst, in_=src)
+            else:
+                nc.vector.tensor_copy(out=dst, in_=src)
+
+        wc_plane_raw = sbuf([P, 1024], U8, "wc_plane_raw")
+        tab_plane = sbuf([P, T], U8, "tab_plane")
+        wb_plane = sbuf([P, N], U8, "wb_plane")
+        nc.vector.memset(tab_plane[:].bitcast(I32), 0)
+        nc.vector.memset(wc_plane_raw[:].bitcast(I32), 0)
+        nc.vector.memset(wb_plane[:].bitcast(I32), 0)
+
+        wc_raw = sbuf([P, 2048], U8, "wc_raw")
+        nc.sync.dma_start(out=wc_raw[:].bitcast(I32), in_=wc_words[0].bitcast(I32))
+        offs_sb = sbuf([P, S // 16], U16, "offs_sb")
+        nc.sync.dma_start(offs_sb[:], offs)
+
+        def load_table(a):
+            words = sbuf([P, T], I32, "tab%d" % a, tag="big", bufs=3)
+            nc.sync.dma_start(out=words[:], in_=tab_words[a].rearrange("p t i -> p (t i)").bitcast(I32))
+            return words
+
+        def load_rows(src, r0, c0, width, name, tag=None, bufs=1):
+            raw = sbuf([P, PACK, width], F32, name, tag=tag, bufs=bufs)
+            nc.sync.dma_start(out=raw[:], in_=src[r0 : r0 + KP, c0 : c0 + width].rearrange("(p j) c -> p j c", j=PACK))
+            return raw
+
+        tab = [load_table(0)]
+        for q in range(4):
+            nc.sync.dma_start(
+                out=tab_plane[32 * q : 32 * q + 12, :].bitcast(I32), in_=tab_scales[:, 4 * q : 4 * q + 4, :].bitcast(I32)
+            )
+        wf00 = load_rows(wf, 0, 0, 512, "wf00")
+        tab.append(load_table(1))
+        for q in range(4):
+            nc.sync.dma_start(
+                out=wc_plane_raw[32 * q : 32 * q + 4, :].bitcast(I32), in_=wc_scales[0, 4 * q : 4 * q + 4, :].bitcast(I32)
+            )
+        tab.append(load_table(2))
+        pos1_sb = sbuf([P, M // 16], U16, "pos1_sb")
+        nc.sync.dma_start(pos1_sb[:], pos1)
+        pos2_sb = sbuf([P, M // 16], U16, "pos2_sb")
+        nc.sync.dma_start(pos2_sb[:], pos2)
+        gain_sb = sbuf([P, 2, PACK], F32, "gain_sb")
+        nc.sync.dma_start(out=gain_sb[:], in_=gain.rearrange("(b p t) -> p b t", b=2, t=PACK))
+        wf01 = [load_rows(wf, KP, 256 * u, 256, "wf01_%d" % u) for u in range(2)]
+        base_sb = [load_rows(base, 0, 0, M, "base0")]
+        wf10 = load_rows(wf, 0, 512, 512, "wf10")
+        wf11 = load_rows(wf, KP, 512, 512, "wf11")
+
+        wc_codes = sbuf([P, 2048], U8, "wc_codes")
+        nc.vector.tensor_copy(
+            out=wc_codes[:].rearrange("p (b t m e) -> p b t m e", b=2, t=PACK, e=2),
+            in_=wc_raw[:].rearrange("p (b m t e) -> p b t m e", b=2, t=PACK, e=2),
+        )
+        def gather_table(a):
+            picked = sbuf([P, S], U32, "v%d" % a)
+            nc.vector.tensor_copy(out=picked[:], in_=tab[a][:].bitcast(U32).indirect(offs_sb[:]))
+            return picked
+
+        def wf_tiles(name):
+            grouped = sbuf([P, 2048], BF16, name + "_g", tag="wfg", bufs=2)
+            codes = sbuf([P, 512], U32, name + "_c")
+            plane = sbuf([P, 512], U8, name + "_s")
+            return grouped, codes, plane
+
+        def cast_wf(engine, grouped, raw, m0, c0, width):
+            dst = grouped.rearrange("p (t m j) -> p m j t", t=PACK, j=PACK)[:, m0 : m0 + width // PACK]
+            cast(engine, dst, raw[:, :, c0 : c0 + width].rearrange("p j (m t) -> p m j t", t=PACK))
+
+        v = [gather_table(0)]
+        v_plane = sbuf([P, S], U8, "v_plane")
+        nc.vector.tensor_copy(out=v_plane[:], in_=tab_plane[:].indirect(offs_sb[:]))
+
+        wfq = {}
+        wfq[0, 0] = wf_tiles("wf00")
+        cast_wf("S", wfq[0, 0][0][:], wf00, 0, 0, 512)
+        quantise(wfq[0, 0][0][:], wfq[0, 0][1][:], wfq[0, 0][2][:])
+        v.append(gather_table(1))
+        wc_plane = sbuf([P, 1024], U8, "wc_plane")
+        nc.vector.tensor_copy(
+            out=wc_plane[:].rearrange("p (b t m) -> p b t m", b=2, t=PACK),
+            in_=wc_plane_raw[:].rearrange("p (b m t) -> p b t m", b=2, t=PACK),
+        )
+
+        v.append(gather_table(2))
+        wa_raw = [load_rows(wa, KP * b, 0, N, "wa%d" % b, tag="big", bufs=3) for b in range(2)]
+        base_sb.append(load_rows(base, KP, 0, M, "base1", tag="big", bufs=3))
+        wb_codes = sbuf([P, 2, N], I32, "wb_codes", tag="wf00")
+        nc.sync.dma_start(out=wb_codes[:], in_=wb_words.rearrange("a p c i -> p a (c i)").bitcast(I32))
+        for q in range(4):
+            nc.sync.dma_start(
+                out=wb_plane[32 * q : 32 * q + 8, :].bitcast(I32), in_=wb_scales[:, 4 * q : 4 * q + 4, :].bitcast(I32)
+            )
+        shift_sb = sbuf([P, 4], F32, "shift_sb")
+        with nc.allow_non_contiguous_dma(reason="one shift value for each output row"):
+            nc.sync.dma_start(out=shift_sb[:], in_=shift.rearrange("(n p) -> p n", p=P))
+
+        def stage1_pass(bank, b, t, half, a):
+            cols = slice(512 * half, 512 * half + 512)
+            w = slice(128 * t, 128 * t + 128)
+            if a == 0:
+                c = 4 * b + t
+                lhsT = wc_codes[:, 256 * c : 256 * c + 256].bitcast(FP4X4)
+                lhsT_scale = wc_plane[:, 128 * c : 128 * c + 128]
+            else:
+                lhsT = wfq[b, a - 1][1][:, w].bitcast(FP8X4)
+                lhsT_scale = wfq[b, a - 1][2][:, w]
+            nc.tensor.matmul_mx(
+                out=bank[:], lhsT=lhsT, lhsT_scale=lhsT_scale,
+                rhs=v[a][:, cols].bitcast(FP8X4), rhs_scale=v_plane[4 * a : P, cols],
+                start=(a == 0), stop=(a == 2),
+            )
+
+        h = {}
+
+        def features(b, t, banks):
+            h[b, t] = sbuf([P, S], F32, "h%d%d" % (b, t), tag="h", bufs=8)
+            g = gain_sb[:, b, t : t + 1]
+            engine = GAIN_ENGINE[4 * b + t]
+            for half in range(2):
+                cols = slice(512 * half, 512 * half + 512)
+                nc.scalar.activation(out=h[b, t][:, cols], in_=banks[half][:], func=ACT.Tanh)
+                if engine == "V" and b + t == 0:
+                    nc.vector.tensor_scalar(out=h[b, t][:, cols], in0=h[b, t][:, cols], scalar1=g, scalar2=None, op0=ALU.mult)
+            if engine == "V" and b + t > 0:
+                nc.vector.tensor_scalar(out=h[b, t][:], in0=h[b, t][:], scalar1=g, scalar2=None, op0=ALU.mult)
+            if engine == "S":
+                nc.scalar.activation(out=h[b, t][:], in_=h[b, t][:], func=ACT.Copy, scale=g)
+            if engine == "G":
+                nc.gpsimd.tensor_scalar(
+                    out=h[b, t][:], in0=h[b, t][:], scalar1=g, scalar2=0.0, op0=ALU.mult, op1=ALU.add
+                )
+
+        def pick(dst, b, t, places):
+            nc.vector.tensor_copy(out=dst, in_=h[b, t][:].indirect(places))
+
+        def woven(grouped):
+            return grouped.rearrange("p (c i t) -> p c t i", i=4, t=PACK)
+
+        def rows(raw):
+            return raw.rearrange("p t (c i) -> p c t i", i=4)
+
+        def x_tiles(name, width, tag=None, bufs=1):
+            grouped = sbuf([P, PACK * width], BF16, name + "_g", tag=tag, bufs=bufs)
+            codes = sbuf([P, width], U32, name + "_c")
+            plane = sbuf([P, width], U8, name + "_s")
+            return grouped, codes, plane
+
+        banks = {}
+        for t in range(PACK):
+            for half in range(2):
+                banks[t, half] = psum.tile([P, 512], F32, name="e0%d%d" % (t, half), tag="bank")
+        for a in range(2):
+            for t in range(PACK):
+                for half in range(2):
+                    stage1_pass(banks[t, half], 0, t, half, a)
+        wfq[0, 1] = wf_tiles("wf01")
+        cast_wf("S", wfq[0, 1][0][:], wf01[0], 0, 0, 256)
+        cast_wf("V", wfq[0, 1][0][:], wf01[1], 64, 0, 256)
+        quantise(wfq[0, 1][0][:, 0:512], wfq[0, 1][1][:, 0:128], wfq[0, 1][2][:, 0:128])
+        quantise(wfq[0, 1][0][:, 512:2048], wfq[0, 1][1][:, 128:512], wfq[0, 1][2][:, 128:512])
+        for t in range(PACK):
+            for half in range(2):
+                stage1_pass(banks[t, half], 0, t, half, 2)
+
+        picked1 = sbuf([P, PACK, M], F32, "picked1_0", tag="picked1")
+        for t in range(PACK):
+            features(0, t, [banks[t, 0], banks[t, 1]])
+            pick(picked1[:, t, :], 0, t, pos1_sb[:])
+
+        for a, raw in enumerate((wf10, wf11)):
+            grouped = sbuf([P, 2048], BF16, "wf1%d_g" % a, tag=("wfg", "picked2")[a], bufs=2 - a)
+            codes = sbuf([P, 512], U32, "wf1%d_c" % a)
+            plane = sbuf([P, 512], U8, "wf1%d_s" % a)
+            wfq[1, a] = (grouped[:], codes, plane)
+            cast_wf("S", wfq[1, a][0], raw, 0, 0, 512)
+            quantise(wfq[1, a][0], codes[:], plane[:])
+        for t in range(PACK):
+            for half in range(2):
+                banks[t, half] = psum.tile([P, 512], F32, name="e1%d%d" % (t, half), tag="bank")
+                for a in range(3):
+                    stage1_pass(banks[t, half], 1, t, half, a)
+
+        xa = [x_tiles("xa0", M, "xg", 3)]
+        nc.vector.tensor_tensor(out=woven(xa[0][0][:]), in0=rows(picked1[:]), in1=rows(base_sb[0][:]), op=ALU.add)
+        quantise(xa[0][0][:], xa[0][1][:], xa[0][2][:])
+        picked2_0 = sbuf([P, PACK, M], F32, "picked2_0", tag="picked2")
+        for t in range(PACK):
+            pick(picked2_0[:, t, :], 0, t, pos2_sb[:])
+
+        waq = []
+        for b in range(2):
+            waq.append(x_tiles("wa%d" % b, N, "xg", 3))
+            cast("S", woven(waq[b][0][:]), rows(wa_raw[b][:]))
+            quantise(waq[b][0][:], waq[b][1][:], waq[b][2][:])
+
+        def places2(i):
+            m0, width = PIECES[i]
+            return pos2_sb[:, m0 // 16 : (m0 + width) // 16]
+
+        picked1 = sbuf([P, PACK, M], F32, "picked1_1", tag="picked1")
+        picked2 = [sbuf([P, PACK, PIECES[0][1]], F32, "picked2_10")]
+        for t in range(PACK):
+            features(1, t, [banks[t, 0], banks[t, 1]])
+            pick(picked1[:, t, :], 1, t, pos1_sb[:])
+            pick(picked2[0][:, t, :], 1, t, places2(0))
+
+        xb0 = x_tiles("xb0", M, "wf11_c")
+        nc.scalar.activation(out=woven(xb0[0][:]), in_=rows(picked2_0[:]), func=ACT.Abs)
+        xa.append(x_tiles("xa1", M, "xg", 3))
+        nc.vector.tensor_tensor(out=woven(xa[1][0][:]), in0=rows(picked1[:]), in1=rows(base_sb[1][:]), op=ALU.add)
+        xb1 = [x_tiles("xb10", PIECES[0][1], "last")]
+
+        def weave_xb(i):
+            nc.scalar.activation(out=woven(xb1[i][0][:]), in_=rows(picked2[i][:]), func=ACT.Abs)
+
+        weave_xb(0)
+        quantise(xb0[0][:], xb0[1][:], xb0[2][:])
+        quantise(xa[1][0][:], xa[1][1][:], xa[1][2][:])
+        quantise(xb1[0][0][:], xb1[0][1][:], xb1[0][2][:])
+
+        ya_sb = sbuf([P, 4, M], F32, "ya_sb", tag="big", bufs=3)
+        ya_banks = [psum.tile([P, M], F32, name="ya%d" % n, tag="bank") for n in range(4)]
+        yb_banks = [psum.tile([P, 512], F32, name="yb%d" % i, tag="bank") for i in range(4)]
+
+        def ya_pass(b):
+            for n in range(4):
+                w = slice(128 * n, 128 * n + 128)
+                nc.tensor.matmul_mx(
+                    out=ya_banks[n][:], lhsT=waq[b][1][:, w].bitcast(FP8X4), lhsT_scale=waq[b][2][:, w],
+                    rhs=xa[b][1][:].bitcast(FP8X4), rhs_scale=xa[b][2][:], start=(b == 0), stop=(b == 1),
+                )
+
+        def yb_place(i, n):
+            m0, width = PIECES[i]
+            c = 4 * m0 + n * width
+            return yb_banks[c // 512][:, c % 512 : c % 512 + width], c % 512 == 0, (c + width) % 512 == 0
+
+        def yb_pass(b, i, codes, plane):
+            for n in range(4):
+                w = slice(128 * n, 128 * n + 128)
+                place, first, last = yb_place(i, n)
+                nc.tensor.matmul_mx(
+                    out=place, lhsT=wb_codes[:, b, w].bitcast(FP8X4), lhsT_scale=wb_plane[4 * b : P, w],
+                    rhs=codes.bitcast(FP8X4), rhs_scale=plane, start=(b == 0 and first), stop=(b == 1 and last),
+                )
+
+        ya_pass(0)
+        ya_pass(1)
+        for i, (m0, width) in enumerate(PIECES):
+            yb_pass(0, i, xb0[1][:, m0 : m0 + width], xb0[2][:, m0 : m0 + width])
+        yb_pass(1, 0, xb1[0][1][:], xb1[0][2][:])
+
+        for i, tag in ((1, "picked1"), (2, "last")):
+            picked2.append(sbuf([P, PACK, PIECES[i][1]], F32, "picked2_1%d" % i, tag=tag))
+            xb1.append(x_tiles("xb1%d" % i, PIECES[i][1]))
+            for t in range(PACK):
+                pick(picked2[i][:, t, :], 1, t, places2(i))
+            weave_xb(i)
+        for n in range(4):
+            nc.scalar.activation(out=ya_sb[:, n, :], in_=ya_banks[n][:], func=ACT.Identity, bias=shift_sb[:, n : n + 1])
+
+        out_rows = out.rearrange("(n p) m -> p n m", p=P)
+
+        def finish(i):
+            m0, width = PIECES[i]
+            scores = sbuf([P, 4, width], F32, "scores%d" % i)
+            for n in range(4):
+                nc.vector.scalar_tensor_tensor(
+                    out=scores[:, n, :], in0=yb_place(i, n)[0], scalar=shift_sb[:, n : n + 1],
+                    in1=ya_sb[:, n, m0 : m0 + width], op0=ALU.add, op1=ALU.max,
+                )
+            nc.sync.dma_start(out=out_rows[:, :, m0 : m0 + width], in_=scores[:])
+
+        quantise(xb1[1][0][:], xb1[1][1][:], xb1[1][2][:])
+        yb_pass(1, 1, xb1[1][1][:], xb1[1][2][:])
+        quantise(xb1[2][0][:], xb1[2][1][:], xb1[2][2][:])
+        yb_pass(1, 2, xb1[2][1][:], xb1[2][2][:])
+        for i in range(3):
+            finish(i)

@@ -50,7 +50,15 @@ def tile_list_clot_lysis_scores_kernel(
         tab_plane = sbuf([P, T], U8, "tab_plane")
         wb_plane = sbuf([P, N], U8, "wb_plane")
         nc.vector.memset(tab_plane[:].bitcast(I32), 0)
+        for q in range(4):
+            nc.gpsimd.dma_start(
+                out=tab_plane[32 * q : 32 * q + 12, :].bitcast(I32), in_=tab_scales[:, 4 * q : 4 * q + 4, :].bitcast(I32)
+            )
         nc.vector.memset(wc_plane_raw[:].bitcast(I32), 0)
+        for q in range(4):
+            nc.gpsimd.dma_start(
+                out=wc_plane_raw[32 * q : 32 * q + 4, :].bitcast(I32), in_=wc_scales[0, 4 * q : 4 * q + 4, :].bitcast(I32)
+            )
         nc.vector.memset(wb_plane[:].bitcast(I32), 0)
 
         wc_raw = sbuf([P, 2048], U8, "wc_raw")
@@ -69,23 +77,15 @@ def tile_list_clot_lysis_scores_kernel(
             return raw
 
         tab = [load_table(0)]
-        for q in range(4):
-            nc.sync.dma_start(
-                out=tab_plane[32 * q : 32 * q + 12, :].bitcast(I32), in_=tab_scales[:, 4 * q : 4 * q + 4, :].bitcast(I32)
-            )
         wf00 = load_rows(wf, 0, 0, 512, "wf00")
-        tab.append(load_table(1))
-        for q in range(4):
-            nc.sync.dma_start(
-                out=wc_plane_raw[32 * q : 32 * q + 4, :].bitcast(I32), in_=wc_scales[0, 4 * q : 4 * q + 4, :].bitcast(I32)
-            )
-        tab.append(load_table(2))
         pos1_sb = sbuf([P, M // 16], U16, "pos1_sb")
         nc.sync.dma_start(pos1_sb[:], pos1)
         pos2_sb = sbuf([P, M // 16], U16, "pos2_sb")
         nc.sync.dma_start(pos2_sb[:], pos2)
         gain_sb = sbuf([P, 2, PACK], F32, "gain_sb")
         nc.sync.dma_start(out=gain_sb[:], in_=gain.rearrange("(b p t) -> p b t", b=2, t=PACK))
+        tab.append(load_table(1))
+        tab.append(load_table(2))
         wf01 = [load_rows(wf, KP, 256 * u, 256, "wf01_%d" % u) for u in range(2)]
         base_sb = [load_rows(base, 0, 0, M, "base0")]
         wf10 = load_rows(wf, 0, 512, 512, "wf10")
@@ -108,8 +108,8 @@ def tile_list_clot_lysis_scores_kernel(
             return grouped, codes, plane
 
         def cast_wf(engine, grouped, raw, m0, c0, width):
-            dst = grouped.rearrange("p (t m j) -> p m j t", t=PACK, j=PACK)[:, m0 : m0 + width // PACK]
-            cast(engine, dst, raw[:, :, c0 : c0 + width].rearrange("p j (m t) -> p m j t", t=PACK))
+            dst = grouped.rearrange("p (u e m j) -> p u m j e", u=2, e=2, j=PACK)[:, :, m0 : m0 + width // PACK]
+            cast(engine, dst, raw[:, :, c0 : c0 + width].rearrange("p j (m u e) -> p u m j e", u=2, e=2))
 
         v = [gather_table(0)]
         v_plane = sbuf([P, S], U8, "v_plane")
@@ -119,13 +119,13 @@ def tile_list_clot_lysis_scores_kernel(
         wfq[0, 0] = wf_tiles("wf00")
         cast_wf("S", wfq[0, 0][0][:], wf00, 0, 0, 512)
         quantise(wfq[0, 0][0][:], wfq[0, 0][1][:], wfq[0, 0][2][:])
-        v.append(gather_table(1))
         wc_plane = sbuf([P, 1024], U8, "wc_plane")
         nc.vector.tensor_copy(
             out=wc_plane[:].rearrange("p (b t m) -> p b t m", b=2, t=PACK),
             in_=wc_plane_raw[:].rearrange("p (b m t) -> p b t m", b=2, t=PACK),
         )
 
+        v.append(gather_table(1))
         v.append(gather_table(2))
         wa_raw = [load_rows(wa, KP * b, 0, N, "wa%d" % b, tag="big", bufs=3) for b in range(2)]
         base_sb.append(load_rows(base, KP, 0, M, "base1", tag="big", bufs=3))
@@ -179,10 +179,10 @@ def tile_list_clot_lysis_scores_kernel(
             nc.vector.tensor_copy(out=dst, in_=h[b, t][:].indirect(places))
 
         def woven(grouped):
-            return grouped.rearrange("p (c i t) -> p c t i", i=4, t=PACK)
+            return grouped.rearrange("p (c i t) -> p c t i", i=2, t=PACK)
 
         def rows(raw):
-            return raw.rearrange("p t (c i) -> p c t i", i=4)
+            return raw.rearrange("p t (c i) -> p c t i", i=2)
 
         def x_tiles(name, width, tag=None, bufs=1):
             grouped = sbuf([P, PACK * width], BF16, name + "_g", tag=tag, bufs=bufs)

@@ -22,7 +22,7 @@ T = 4096
 S = 1024
 M = 512
 N = 512
-GAIN_ENGINE = "VVVVSSSS"
+GAIN_ENGINE = "VGGGSSSG"
 PIECES = ((0, 256), (256, 128), (384, 128))
 
 
@@ -166,14 +166,14 @@ def tile_list_clot_lysis_scores_kernel(
                 nc.scalar.activation(out=h[b, t][:, cols], in_=banks[half][:], func=ACT.Tanh)
                 if engine == "V" and b + t == 0:
                     nc.vector.tensor_scalar(out=h[b, t][:, cols], in0=h[b, t][:, cols], scalar1=g, scalar2=None, op0=ALU.mult)
+                if engine == "G":
+                    nc.gpsimd.tensor_scalar(
+                        out=h[b, t][:, cols], in0=h[b, t][:, cols], scalar1=g, scalar2=0.0, op0=ALU.mult, op1=ALU.add
+                    )
             if engine == "V" and b + t > 0:
                 nc.vector.tensor_scalar(out=h[b, t][:], in0=h[b, t][:], scalar1=g, scalar2=None, op0=ALU.mult)
             if engine == "S":
                 nc.scalar.activation(out=h[b, t][:], in_=h[b, t][:], func=ACT.Copy, scale=g)
-            if engine == "G":
-                nc.gpsimd.tensor_scalar(
-                    out=h[b, t][:], in0=h[b, t][:], scalar1=g, scalar2=0.0, op0=ALU.mult, op1=ALU.add
-                )
 
         def pick(dst, b, t, places):
             nc.vector.tensor_copy(out=dst, in_=h[b, t][:].indirect(places))
@@ -184,9 +184,9 @@ def tile_list_clot_lysis_scores_kernel(
         def rows(raw):
             return raw.rearrange("p t (c i) -> p c t i", i=2)
 
-        def x_tiles(name, width, tag=None, bufs=1):
+        def x_tiles(name, width, tag=None, bufs=1, codes_tag=None):
             grouped = sbuf([P, PACK * width], BF16, name + "_g", tag=tag, bufs=bufs)
-            codes = sbuf([P, width], U32, name + "_c")
+            codes = sbuf([P, width], U32, name + "_c", tag=codes_tag)
             plane = sbuf([P, width], U8, name + "_s")
             return grouped, codes, plane
 
@@ -200,7 +200,8 @@ def tile_list_clot_lysis_scores_kernel(
                     stage1_pass(banks[t, half], 0, t, half, a)
         wfq[0, 1] = wf_tiles("wf01")
         cast_wf("S", wfq[0, 1][0][:], wf01[0], 0, 0, 256)
-        cast_wf("V", wfq[0, 1][0][:], wf01[1], 64, 0, 256)
+        cast_wf("S", wfq[0, 1][0][:], wf01[1], 64, 0, 128)
+        cast_wf("V", wfq[0, 1][0][:], wf01[1], 96, 128, 128)
         quantise(wfq[0, 1][0][:, 0:512], wfq[0, 1][1][:, 0:128], wfq[0, 1][2][:, 0:128])
         quantise(wfq[0, 1][0][:, 512:2048], wfq[0, 1][1][:, 128:512], wfq[0, 1][2][:, 128:512])
         for t in range(PACK):
@@ -208,50 +209,65 @@ def tile_list_clot_lysis_scores_kernel(
                 stage1_pass(banks[t, half], 0, t, half, 2)
 
         picked1 = sbuf([P, PACK, M], F32, "picked1_0", tag="picked1")
-        for t in range(PACK):
+        picked2_0 = sbuf([P, PACK, M], F32, "picked2_0")
+
+        def first_half(t):
             features(0, t, [banks[t, 0], banks[t, 1]])
             pick(picked1[:, t, :], 0, t, pos1_sb[:])
 
-        for a, raw in enumerate((wf10, wf11)):
-            grouped = sbuf([P, 2048], BF16, "wf1%d_g" % a, tag=("wfg", "picked2")[a], bufs=2 - a)
-            codes = sbuf([P, 512], U32, "wf1%d_c" % a)
-            plane = sbuf([P, 512], U8, "wf1%d_s" % a)
-            wfq[1, a] = (grouped[:], codes, plane)
-            cast_wf("S", wfq[1, a][0], raw, 0, 0, 512)
-            quantise(wfq[1, a][0], codes[:], plane[:])
+        def quantise_wf1(a, raw, grouped):
+            wfq[1, a] = (grouped, sbuf([P, 512], U32, "wf1%d_c" % a), sbuf([P, 512], U8, "wf1%d_s" % a))
+            cast_wf("S", grouped, raw, 0, 0, 512)
+            quantise(grouped, wfq[1, a][1][:], wfq[1, a][2][:])
+
+        for t in range(2):
+            first_half(t)
+            pick(picked2_0[:, t, :], 0, t, pos2_sb[:])
+        wf10_g = sbuf([P, 2048], BF16, "wf10_g", tag="wfg", bufs=2)
+        quantise_wf1(0, wf10, wf10_g[:])
+        first_half(2)
+        quantise_wf1(1, wf11, picked2_0[:, 2:4, :].rearrange("p t m -> p (t m)").bitcast(BF16))
+        pick(picked2_0[:, 2, :], 0, 2, pos2_sb[:])
+        first_half(3)
+        pick(picked2_0[:, 3, :], 0, 3, pos2_sb[:])
+
         for t in range(PACK):
             for half in range(2):
                 banks[t, half] = psum.tile([P, 512], F32, name="e1%d%d" % (t, half), tag="bank")
                 for a in range(3):
                     stage1_pass(banks[t, half], 1, t, half, a)
 
-        xa = [x_tiles("xa0", M, "xg", 3)]
-        nc.vector.tensor_tensor(out=woven(xa[0][0][:]), in0=rows(picked1[:]), in1=rows(base_sb[0][:]), op=ALU.add)
-        quantise(xa[0][0][:], xa[0][1][:], xa[0][2][:])
-        picked2_0 = sbuf([P, PACK, M], F32, "picked2_0", tag="picked2")
-        for t in range(PACK):
-            pick(picked2_0[:, t, :], 0, t, pos2_sb[:])
+        xa0_g = sbuf([P, PACK * M], BF16, "xa0_g")
+        for u in range(4):
+            nc.gpsimd.tensor_tensor(
+                out=woven(xa0_g[:, 512 * u : 512 * u + 512]), in0=rows(picked1[:, :, 128 * u : 128 * u + 128]),
+                in1=rows(base_sb[0][:, :, 128 * u : 128 * u + 128]), op=ALU.add,
+            )
 
         waq = []
-        for b in range(2):
-            waq.append(x_tiles("wa%d" % b, N, "xg", 3))
-            cast("S", woven(waq[b][0][:]), rows(wa_raw[b][:]))
-            quantise(waq[b][0][:], waq[b][1][:], waq[b][2][:])
+
+        def cast_wa(b, c0, width):
+            cast("S", woven(waq[b][0][:, PACK * c0 : PACK * (c0 + width)]), rows(wa_raw[b][:, :, c0 : c0 + width]))
+
+        waq.append(x_tiles("wa0", N))
+        cast_wa(0, 0, 256)
 
         def places2(i):
             m0, width = PIECES[i]
             return pos2_sb[:, m0 // 16 : (m0 + width) // 16]
 
-        picked1 = sbuf([P, PACK, M], F32, "picked1_1", tag="picked1")
+        picked1 = sbuf([P, PACK, M], F32, "picked1_1", tag="wf10")
         picked2 = [sbuf([P, PACK, PIECES[0][1]], F32, "picked2_10")]
         for t in range(PACK):
             features(1, t, [banks[t, 0], banks[t, 1]])
             pick(picked1[:, t, :], 1, t, pos1_sb[:])
             pick(picked2[0][:, t, :], 1, t, places2(0))
 
+        cast_wa(0, 256, 256)
+        quantise(waq[0][0][:], waq[0][1][:], waq[0][2][:])
         xb0 = x_tiles("xb0", M, "wf11_c")
         nc.scalar.activation(out=woven(xb0[0][:]), in_=rows(picked2_0[:]), func=ACT.Abs)
-        xa.append(x_tiles("xa1", M, "xg", 3))
+        xa = [(xa0_g, sbuf([P, M], U32, "xa0_c", tag="picked2_0"), sbuf([P, M], U8, "xa0_s")), x_tiles("xa1", M)]
         nc.vector.tensor_tensor(out=woven(xa[1][0][:]), in0=rows(picked1[:]), in1=rows(base_sb[1][:]), op=ALU.add)
         xb1 = [x_tiles("xb10", PIECES[0][1], "last")]
 
@@ -259,7 +275,11 @@ def tile_list_clot_lysis_scores_kernel(
             nc.scalar.activation(out=woven(xb1[i][0][:]), in_=rows(picked2[i][:]), func=ACT.Abs)
 
         weave_xb(0)
+        quantise(xa[0][0][:], xa[0][1][:], xa[0][2][:])
         quantise(xb0[0][:], xb0[1][:], xb0[2][:])
+        waq.append(x_tiles("wa1", N, "wf10_c"))
+        cast_wa(1, 0, N)
+        quantise(waq[1][0][:], waq[1][1][:], waq[1][2][:])
         quantise(xa[1][0][:], xa[1][1][:], xa[1][2][:])
         quantise(xb1[0][0][:], xb1[0][1][:], xb1[0][2][:])
 
@@ -290,19 +310,23 @@ def tile_list_clot_lysis_scores_kernel(
                 )
 
         ya_pass(0)
-        ya_pass(1)
         for i, (m0, width) in enumerate(PIECES):
             yb_pass(0, i, xb0[1][:, m0 : m0 + width], xb0[2][:, m0 : m0 + width])
+        ya_pass(1)
         yb_pass(1, 0, xb1[0][1][:], xb1[0][2][:])
 
-        for i, tag in ((1, "picked1"), (2, "last")):
+        def empty_ya(n):
+            nc.scalar.activation(out=ya_sb[:, n, :], in_=ya_banks[n][:], func=ACT.Identity, bias=shift_sb[:, n : n + 1])
+
+        empty_ya(0)
+        for i, tag, grouped_tag in ((1, "wf10", "xa1_c"), (2, "last", "wa1_c")):
             picked2.append(sbuf([P, PACK, PIECES[i][1]], F32, "picked2_1%d" % i, tag=tag))
-            xb1.append(x_tiles("xb1%d" % i, PIECES[i][1]))
+            xb1.append(x_tiles("xb1%d" % i, PIECES[i][1], grouped_tag))
             for t in range(PACK):
                 pick(picked2[i][:, t, :], 1, t, places2(i))
+            empty_ya(i)
             weave_xb(i)
-        for n in range(4):
-            nc.scalar.activation(out=ya_sb[:, n, :], in_=ya_banks[n][:], func=ACT.Identity, bias=shift_sb[:, n : n + 1])
+        empty_ya(3)
 
         out_rows = out.rearrange("(n p) m -> p n m", p=P)
 
@@ -314,7 +338,8 @@ def tile_list_clot_lysis_scores_kernel(
                     out=scores[:, n, :], in0=yb_place(i, n)[0], scalar=shift_sb[:, n : n + 1],
                     in1=ya_sb[:, n, m0 : m0 + width], op0=ALU.add, op1=ALU.max,
                 )
-            nc.sync.dma_start(out=out_rows[:, :, m0 : m0 + width], in_=scores[:])
+                if n % 2 == 1:
+                    nc.sync.dma_start(out=out_rows[:, n - 1 : n + 1, m0 : m0 + width], in_=scores[:, n - 1 : n + 1, :])
 
         quantise(xb1[1][0][:], xb1[1][1][:], xb1[1][2][:])
         yb_pass(1, 1, xb1[1][1][:], xb1[1][2][:])

from contextlib import ExitStack

import concourse.mybir as mybir

FLOPS = 4294967296

F32 = mybir.dt.float32
BF16 = mybir.dt.bfloat16
I32 = mybir.dt.int32
U32 = mybir.dt.uint32
U16 = mybir.dt.uint16
U8 = mybir.dt.uint8
FP8X4 = mybir.dt.float8_e4m3fn_x4
FP4X4 = mybir.dt.float4_e2m1fn_x4
ACT = mybir.ActivationFunctionType
ALU = mybir.AluOpType

P = 128
PACK = 4
KP = 512
T = 4096
S = 1024
M = 512
N = 512
GAIN_ENGINE = "VGGGSSSG"
PIECES = ((0, 256), (256, 128), (384, 128))


def tile_list_clot_lysis_scores_kernel(
    tc, tab_words, tab_scales, offs, pos1, pos2, wc_words, wc_scales, wf, gain, base, wa, wb_words, wb_scales, shift, out
):
    nc = tc.nc
    with ExitStack() as ctx:
        keep = ctx.enter_context(tc.tile_pool(name="keep", bufs=1))
        psum = ctx.enter_context(tc.psum_pool(name="psum", bufs=8))

        def sbuf(shape, dtype, name, tag=None, bufs=1):
            return keep.tile(shape, dtype, name=name, tag=tag or name, bufs=bufs, align_bytes=64)

        def quantise(grouped, codes, scales):
            nc.vector.quantize_mx(out=codes.bitcast(FP8X4), scales=scales, in_=grouped)

        def cast(engine, dst, src):
            if engine == "S":
                nc.scalar.copy(out=dst, in_=src)
            else:
                nc.vector.tensor_copy(out=dst, in_=src)

        wc_plane_raw = sbuf([P, 1024], U8, "wc_plane_raw")
        tab_plane = sbuf([P, T], U8, "tab_plane")
        wb_plane = sbuf([P, N], U8, "wb_plane")
        nc.vector.memset(tab_plane[:].bitcast(I32), 0)
        for q in range(4):
            nc.gpsimd.dma_start(
                out=tab_plane[32 * q : 32 * q + 12, :].bitcast(I32), in_=tab_scales[:, 4 * q : 4 * q + 4, :].bitcast(I32)
            )
        nc.vector.memset(wc_plane_raw[:].bitcast(I32), 0)
        for q in range(4):
            nc.gpsimd.dma_start(
                out=wc_plane_raw[32 * q : 32 * q + 4, :].bitcast(I32), in_=wc_scales[0, 4 * q : 4 * q + 4, :].bitcast(I32)
            )
        nc.vector.memset(wb_plane[:].bitcast(I32), 0)

        wc_raw = sbuf([P, 2048], U8, "wc_raw")
        nc.sync.dma_start(out=wc_raw[:].bitcast(I32), in_=wc_words[0].bitcast(I32))
        offs_sb = sbuf([P, S // 16], U16, "offs_sb")
        nc.sync.dma_start(offs_sb[:], offs)

        def load_table(a):
            words = sbuf([P, T], I32, "tab%d" % a, tag="big", bufs=3)
            nc.sync.dma_start(out=words[:], in_=tab_words[a].rearrange("p t i -> p (t i)").bitcast(I32))
            return words

        def load_rows(src, r0, c0, width, name, tag=None, bufs=1):
            raw = sbuf([P, PACK, width], F32, name, tag=tag, bufs=bufs)
            nc.sync.dma_start(out=raw[:], in_=src[r0 : r0 + KP, c0 : c0 + width].rearrange("(p j) c -> p j c", j=PACK))
            return raw

        tab = [load_table(0)]
        wf00 = load_rows(wf, 0, 0, 512, "wf00")
        pos1_sb = sbuf([P, M // 16], U16, "pos1_sb")
        nc.sync.dma_start(pos1_sb[:], pos1)
        pos2_sb = sbuf([P, M // 16], U16, "pos2_sb")
        nc.sync.dma_start(pos2_sb[:], pos2)
        gain_sb = sbuf([P, 2, PACK], F32, "gain_sb")
        nc.sync.dma_start(out=gain_sb[:], in_=gain.rearrange("(b p t) -> p b t", b=2, t=PACK))
        tab.append(load_table(1))
        tab.append(load_table(2))
        wf01 = [load_rows(wf, KP, 256 * u, 256, "wf01_%d" % u) for u in range(2)]
        base_sb = [load_rows(base, 0, 0, M, "base0")]
        wf10 = load_rows(wf, 0, 512, 512, "wf10")
        wf11 = load_rows(wf, KP, 512, 512, "wf11")

        wc_codes = sbuf([P, 2048], U8, "wc_codes")
        nc.vector.tensor_copy(
            out=wc_codes[:].rearrange("p (b t m e) -> p b t m e", b=2, t=PACK, e=2),
            in_=wc_raw[:].rearrange("p (b m t e) -> p b t m e", b=2, t=PACK, e=2),
        )
        def gather_table(a):
            picked = sbuf([P, S], U32, "v%d" % a)
            nc.vector.tensor_copy(out=picked[:], in_=tab[a][:].bitcast(U32).indirect(offs_sb[:]))
            return picked

        def wf_tiles(name):
            grouped = sbuf([P, 2048], BF16, name + "_g", tag="wfg", bufs=2)
            codes = sbuf([P, 512], U32, name + "_c")
            plane = sbuf([P, 512], U8, name + "_s")
            return grouped, codes, plane

        def cast_wf(engine, grouped, raw, m0, c0, width):
            dst = grouped.rearrange("p (u e m j) -> p u m j e", u=2, e=2, j=PACK)[:, :, m0 : m0 + width // PACK]
            cast(engine, dst, raw[:, :, c0 : c0 + width].rearrange("p j (m u e) -> p u m j e", u=2, e=2))

        v = [gather_table(0)]
        v_plane = sbuf([P, S], U8, "v_plane")
        nc.vector.tensor_copy(out=v_plane[:], in_=tab_plane[:].indirect(offs_sb[:]))

        wfq = {}
        wfq[0, 0] = wf_tiles("wf00")
        cast_wf("S", wfq[0, 0][0][:], wf00, 0, 0, 512)
        quantise(wfq[0, 0][0][:], wfq[0, 0][1][:], wfq[0, 0][2][:])
        wc_plane = sbuf([P, 1024], U8, "wc_plane")
        nc.vector.tensor_copy(
            out=wc_plane[:].rearrange("p (b t m) -> p b t m", b=2, t=PACK),
            in_=wc_plane_raw[:].rearrange("p (b m t) -> p b t m", b=2, t=PACK),
        )

        v.append(gather_table(1))
        v.append(gather_table(2))
        wa_raw = [load_rows(wa, KP * b, 0, N, "wa%d" % b, tag="big", bufs=3) for b in range(2)]
        base_sb.append(load_rows(base, KP, 0, M, "base1", tag="big", bufs=3))
        wb_codes = sbuf([P, 2, N], I32, "wb_codes", tag="wf00")
        nc.sync.dma_start(out=wb_codes[:], in_=wb_words.rearrange("a p c i -> p a (c i)").bitcast(I32))
        for q in range(4):
            nc.sync.dma_start(
                out=wb_plane[32 * q : 32 * q + 8, :].bitcast(I32), in_=wb_scales[:, 4 * q : 4 * q + 4, :].bitcast(I32)
            )
        shift_sb = sbuf([P, 4], F32, "shift_sb")
        with nc.allow_non_contiguous_dma(reason="one shift value for each output row"):
            nc.sync.dma_start(out=shift_sb[:], in_=shift.rearrange("(n p) -> p n", p=P))

        def stage1_pass(bank, b, t, half, a):
            cols = slice(512 * half, 512 * half + 512)
            w = slice(128 * t, 128 * t + 128)
            if a == 0:
                c = 4 * b + t
                lhsT = wc_codes[:, 256 * c : 256 * c + 256].bitcast(FP4X4)
                lhsT_scale = wc_plane[:, 128 * c : 128 * c + 128]
            else:
                lhsT = wfq[b, a - 1][1][:, w].bitcast(FP8X4)
                lhsT_scale = wfq[b, a - 1][2][:, w]
            nc.tensor.matmul_mx(
                out=bank[:], lhsT=lhsT, lhsT_scale=lhsT_scale,
                rhs=v[a][:, cols].bitcast(FP8X4), rhs_scale=v_plane[4 * a : P, cols],
                start=(a == 0), stop=(a == 2),
            )

        h = {}

        def features(b, t, banks):
            h[b, t] = sbuf([P, S], F32, "h%d%d" % (b, t), tag="h", bufs=8)
            g = gain_sb[:, b, t : t + 1]
            engine = GAIN_ENGINE[4 * b + t]
            for half in range(2):
                cols = slice(512 * half, 512 * half + 512)
                nc.scalar.activation(out=h[b, t][:, cols], in_=banks[half][:], func=ACT.Tanh)
                if engine == "V" and b + t == 0:
                    nc.vector.tensor_scalar(out=h[b, t][:, cols], in0=h[b, t][:, cols], scalar1=g, scalar2=None, op0=ALU.mult)
                if engine == "G":
                    nc.gpsimd.tensor_scalar(
                        out=h[b, t][:, cols], in0=h[b, t][:, cols], scalar1=g, scalar2=0.0, op0=ALU.mult, op1=ALU.add
                    )
            if engine == "V" and b + t > 0:
                nc.vector.tensor_scalar(out=h[b, t][:], in0=h[b, t][:], scalar1=g, scalar2=None, op0=ALU.mult)
            if engine == "S":
                nc.scalar.activation(out=h[b, t][:], in_=h[b, t][:], func=ACT.Copy, scale=g)

        def pick(dst, b, t, places):
            nc.vector.tensor_copy(out=dst, in_=h[b, t][:].indirect(places))

        def woven(grouped):
            return grouped.rearrange("p (c i t) -> p c t i", i=2, t=PACK)

        def rows(raw):
            return raw.rearrange("p t (c i) -> p c t i", i=2)

        def x_tiles(name, width, tag=None, bufs=1, codes_tag=None):
            grouped = sbuf([P, PACK * width], BF16, name + "_g", tag=tag, bufs=bufs)
            codes = sbuf([P, width], U32, name + "_c", tag=codes_tag)
            plane = sbuf([P, width], U8, name + "_s")
            return grouped, codes, plane

        banks = {}
        for t in range(PACK):
            for half in range(2):
                banks[t, half] = psum.tile([P, 512], F32, name="e0%d%d" % (t, half), tag="bank")
        for a in range(2):
            for t in range(PACK):
                for half in range(2):
                    stage1_pass(banks[t, half], 0, t, half, a)
        wfq[0, 1] = wf_tiles("wf01")
        cast_wf("S", wfq[0, 1][0][:], wf01[0], 0, 0, 256)
        cast_wf("S", wfq[0, 1][0][:], wf01[1], 64, 0, 128)
        cast_wf("V", wfq[0, 1][0][:], wf01[1], 96, 128, 128)
        quantise(wfq[0, 1][0][:, 0:512], wfq[0, 1][1][:, 0:128], wfq[0, 1][2][:, 0:128])
        quantise(wfq[0, 1][0][:, 512:2048], wfq[0, 1][1][:, 128:512], wfq[0, 1][2][:, 128:512])
        for t in range(PACK):
            for half in range(2):
                stage1_pass(banks[t, half], 0, t, half, 2)

        picked1 = sbuf([P, PACK, M], F32, "picked1_0", tag="picked1")
        picked2_0 = sbuf([P, PACK, M], F32, "picked2_0")

        def first_half(t):
            features(0, t, [banks[t, 0], banks[t, 1]])
            pick(picked1[:, t, :], 0, t, pos1_sb[:])

        def quantise_wf1(a, raw, grouped):
            wfq[1, a] = (grouped, sbuf([P, 512], U32, "wf1%d_c" % a), sbuf([P, 512], U8, "wf1%d_s" % a))
            cast_wf("S", grouped, raw, 0, 0, 512)
            quantise(grouped, wfq[1, a][1][:], wfq[1, a][2][:])

        for t in range(2):
            first_half(t)
            pick(picked2_0[:, t, :], 0, t, pos2_sb[:])
        wf10_g = sbuf([P, 2048], BF16, "wf10_g", tag="wfg", bufs=2)
        quantise_wf1(0, wf10, wf10_g[:])
        first_half(2)
        quantise_wf1(1, wf11, picked2_0[:, 2:4, :].rearrange("p t m -> p (t m)").bitcast(BF16))
        pick(picked2_0[:, 2, :], 0, 2, pos2_sb[:])
        first_half(3)
        pick(picked2_0[:, 3, :], 0, 3, pos2_sb[:])

        for t in range(PACK):
            for half in range(2):
                banks[t, half] = psum.tile([P, 512], F32, name="e1%d%d" % (t, half), tag="bank")
                for a in range(3):
                    stage1_pass(banks[t, half], 1, t, half, a)

        xa0_g = sbuf([P, PACK * M], BF16, "xa0_g")
        for u in range(4):
            nc.gpsimd.tensor_tensor(
                out=woven(xa0_g[:, 512 * u : 512 * u + 512]), in0=rows(picked1[:, :, 128 * u : 128 * u + 128]),
                in1=rows(base_sb[0][:, :, 128 * u : 128 * u + 128]), op=ALU.add,
            )

        waq = []

        def cast_wa(b, c0, width):
            cast("S", woven(waq[b][0][:, PACK * c0 : PACK * (c0 + width)]), rows(wa_raw[b][:, :, c0 : c0 + width]))

        waq.append(x_tiles("wa0", N))
        cast_wa(0, 0, 256)

        def places2(i):
            m0, width = PIECES[i]
            return pos2_sb[:, m0 // 16 : (m0 + width) // 16]

        picked1 = sbuf([P, PACK, M], F32, "picked1_1", tag="wf10")
        picked2 = [sbuf([P, PACK, PIECES[0][1]], F32, "picked2_10")]
        for t in range(PACK):
            features(1, t, [banks[t, 0], banks[t, 1]])
            pick(picked1[:, t, :], 1, t, pos1_sb[:])
            pick(picked2[0][:, t, :], 1, t, places2(0))

        cast_wa(0, 256, 256)
        quantise(waq[0][0][:], waq[0][1][:], waq[0][2][:])
        xb0 = x_tiles("xb0", M, "wf11_c")
        nc.scalar.activation(out=woven(xb0[0][:]), in_=rows(picked2_0[:]), func=ACT.Abs)
        xa = [(xa0_g, sbuf([P, M], U32, "xa0_c", tag="picked2_0"), sbuf([P, M], U8, "xa0_s")), x_tiles("xa1", M)]
        nc.vector.tensor_tensor(out=woven(xa[1][0][:]), in0=rows(picked1[:]), in1=rows(base_sb[1][:]), op=ALU.add)
        xb1 = [x_tiles("xb10", PIECES[0][1], "last")]

        def weave_xb(i):
            nc.scalar.activation(out=woven(xb1[i][0][:]), in_=rows(picked2[i][:]), func=ACT.Abs)

        weave_xb(0)
        quantise(xa[0][0][:], xa[0][1][:], xa[0][2][:])
        quantise(xb0[0][:], xb0[1][:], xb0[2][:])
        waq.append(x_tiles("wa1", N, "wf10_c"))
        cast_wa(1, 0, N)
        quantise(waq[1][0][:], waq[1][1][:], waq[1][2][:])
        quantise(xa[1][0][:], xa[1][1][:], xa[1][2][:])
        quantise(xb1[0][0][:], xb1[0][1][:], xb1[0][2][:])

        ya_sb = sbuf([P, 4, M], F32, "ya_sb", tag="big", bufs=3)
        ya_banks = [psum.tile([P, M], F32, name="ya%d" % n, tag="bank") for n in range(4)]
        yb_banks = [psum.tile([P, 512], F32, name="yb%d" % i, tag="bank") for i in range(4)]

        def ya_pass(b):
            for n in range(4):
                w = slice(128 * n, 128 * n + 128)
                nc.tensor.matmul_mx(
                    out=ya_banks[n][:], lhsT=waq[b][1][:, w].bitcast(FP8X4), lhsT_scale=waq[b][2][:, w],
                    rhs=xa[b][1][:].bitcast(FP8X4), rhs_scale=xa[b][2][:], start=(b == 0), stop=(b == 1),
                )

        def yb_place(i, n):
            m0, width = PIECES[i]
            c = 4 * m0 + n * width
            return yb_banks[c // 512][:, c % 512 : c % 512 + width], c % 512 == 0, (c + width) % 512 == 0

        def yb_pass(b, i, codes, plane):
            for n in range(4):
                w = slice(128 * n, 128 * n + 128)
                place, first, last = yb_place(i, n)
                nc.tensor.matmul_mx(
                    out=place, lhsT=wb_codes[:, b, w].bitcast(FP8X4), lhsT_scale=wb_plane[4 * b : P, w],
                    rhs=codes.bitcast(FP8X4), rhs_scale=plane, start=(b == 0 and first), stop=(b == 1 and last),
                )

        ya_pass(0)
        for i, (m0, width) in enumerate(PIECES):
            yb_pass(0, i, xb0[1][:, m0 : m0 + width], xb0[2][:, m0 : m0 + width])
        ya_pass(1)
        yb_pass(1, 0, xb1[0][1][:], xb1[0][2][:])

        def empty_ya(n):
            nc.scalar.activation(out=ya_sb[:, n, :], in_=ya_banks[n][:], func=ACT.Identity, bias=shift_sb[:, n : n + 1])

        empty_ya(0)
        for i, tag, grouped_tag in ((1, "wf10", "xa1_c"), (2, "last", "wa1_c")):
            picked2.append(sbuf([P, PACK, PIECES[i][1]], F32, "picked2_1%d" % i, tag=tag))
            xb1.append(x_tiles("xb1%d" % i, PIECES[i][1], grouped_tag))
            for t in range(PACK):
                pick(picked2[i][:, t, :], 1, t, places2(i))
            empty_ya(i)
            weave_xb(i)
        empty_ya(3)

        out_rows = out.rearrange("(n p) m -> p n m", p=P)

        def finish(i):
            m0, width = PIECES[i]
            scores = sbuf([P, 4, width], F32, "scores%d" % i)
            for n in range(4):
                nc.vector.scalar_tensor_tensor(
                    out=scores[:, n, :], in0=yb_place(i, n)[0], scalar=shift_sb[:, n : n + 1],
                    in1=ya_sb[:, n, m0 : m0 + width], op0=ALU.add, op1=ALU.max,
                )
                if n % 2 == 1:
                    nc.sync.dma_start(out=out_rows[:, n - 1 : n + 1, m0 : m0 + width], in_=scores[:, n - 1 : n + 1, :])

        quantise(xb1[1][0][:], xb1[1][1][:], xb1[1][2][:])
        yb_pass(1, 1, xb1[1][1][:], xb1[1][2][:])
        quantise(xb1[2][0][:], xb1[2][1][:], xb1[2][2][:])
        yb_pass(1, 2, xb1[2][1][:], xb1[2][2][:])
        for i in range(3):
            finish(i)
